import numpy as np
import ml_dtypes


def mxq(x, axis, fmt="e4m3"):
    dtype, down = {"e4m3": (ml_dtypes.float8_e4m3fn, 7), "e5m2": (ml_dtypes.float8_e5m2, 14)}[fmt]
    v = np.moveaxis(np.asarray(x, np.float32).astype(ml_dtypes.bfloat16).astype(np.float64), axis, -1)
    blocks = v.reshape(v.shape[:-1] + (-1, 32))
    amax = np.abs(blocks).max(-1, keepdims=True)
    byte = np.maximum(np.where(amax > 0, np.frexp(amax)[1] - 1 + 127, 0) - down, 1)
    scale = np.exp2(byte - 127.0)
    codes = (blocks / scale).astype(np.float32).astype(dtype).astype(np.float64)
    return np.moveaxis((codes * scale).reshape(v.shape), -1, axis)


WIDE = False


def mx_kscale(k):
    if not WIDE:
        return np.ones(k)
    levels = np.array([10, -10, 5, -5, 0])
    if k % 512:
        return np.exp2(np.random.permutation(np.resize(levels, k // 32))).repeat(32)
    a = np.empty((k // 512, 16))
    for p in range(k // 512):
        a[p, :8] = np.random.permutation(np.resize(levels, 8))
        for g in range(8):
            far = levels[np.abs(levels - a[p, g]) >= 10]
            a[p, g + 8] = far[np.random.randint(len(far))]
    return np.exp2(a.ravel()).repeat(32)


def f64(x):
    return np.asarray(x).astype(np.float64)


def striped8(idx):
    return np.concatenate([x.reshape(-1, 16).T for x in idx]).astype(np.uint16)


def runs(offs, k):
    lists = np.stack([offs[16 * r : 16 * r + 16].T.reshape(-1) for r in range(8)]).astype(np.int64)
    return lists[np.arange(k) % 512 // 64]


def pack_weight(w):
    k, n = w.shape
    w = f64(np.asarray(w, np.float32).astype(ml_dtypes.bfloat16)).reshape(k // 32, 32, n)
    amax = np.abs(w).max(1)
    byte = np.clip(np.where(amax > 0, np.frexp(amax)[1] - 1 + 127 - 7, 1), 1, 254)
    scaled = (w * np.exp2(127.0 - byte)[:, None, :]).reshape(k, n).astype(np.float32)
    words = np.ascontiguousarray(scaled.reshape(k // 512, 128, 4, n).transpose(0, 1, 3, 2)).astype(ml_dtypes.float8_e4m3fn).view(np.uint8)
    return words, np.ascontiguousarray(byte.astype(np.uint8).reshape(k // 512, 16, n))


def unpack_weight(words, scales):
    g, p, n, _ = words.shape
    vals = np.ascontiguousarray(words).view(ml_dtypes.float8_e4m3fn).astype(np.float64) * np.repeat(np.exp2(scales.astype(np.float64) - 127.0), 8, axis=1)[..., None]
    return vals.transpose(0, 1, 3, 2).reshape(g * 512, n)


def sigmoid(v):
    return 1.0 / (1.0 + np.exp(-np.maximum(v, -700.0)))


K, T, S, N, H = 512, 2048, 512, 512, 512


def setup_inputs():
    n = np.random.standard_normal
    s = mx_kscale(K)[:, None]
    u = mx_kscale(H)
    packed_xT = pack_weight(n((K, T)) * s)
    return {
        "x_words": packed_xT[0],
        "x_scales": packed_xT[1],
        "w1": (n((K, H)) / np.sqrt(K) / s).astype(np.float32),
        "gn": (np.random.uniform(0.5, 1.5, (H, 1)) * u[:, None]).astype(np.float32),
        "w2": (n((H, N)) / np.sqrt(H) / u[:, None]).astype(np.float32),
        "offs": striped8(np.random.randint(0, T, (8, S))),
        "n1": striped8(np.stack([np.random.permutation(S) for _ in range(8)])),
        "n2": striped8(np.stack([np.random.permutation(S) for _ in range(8)])),
        "n3": striped8(np.stack([np.random.permutation(S) for _ in range(8)])),
    }


def reference(x_words, x_scales, w1, gn, w2, offs, n1, n2, n3):
    xq = unpack_weight(x_words, x_scales)[np.arange(K)[:, None], runs(offs, K)]
    y = mxq(f64(w1), 0, "e4m3").T @ xq
    z = f64(gn) * (np.maximum(y, y[np.arange(H)[:, None], runs(n1, H)]))
    h = mxq(f64(w2), 0, "e4m3").T @ mxq(z, 0, "e4m3")
    return (h - (h[np.arange(N)[:, None], runs(n2, N)])) * (sigmoid(h[np.arange(N)[:, None], runs(n3, N)]))

@@ -1,0 +1,156 @@
+from contextlib import ExitStack
+
+import concourse.mybir as mybir
+
+K, T, S, N, H = 512, 2048, 512, 512, 512
+FLOPS = 2 * K * H * S + 2 * H * N * S
+
+F32 = mybir.dt.float32
+BF16 = mybir.dt.bfloat16
+I32 = mybir.dt.int32
+U32 = mybir.dt.uint32
+U16 = mybir.dt.uint16
+U8 = mybir.dt.uint8
+FP8X4 = mybir.dt.float8_e4m3fn_x4
+ALU = mybir.AluOpType
+ACT = mybir.ActivationFunctionType
+
+P = 128
+PACK = 4
+HALF = S // 2
+FETCH_PIECES = ((0, 384), (384, 512))
+Z_PIECES = ((0, 256), (256, 384), (384, 512))
+
+
+def entries(lst, lo, hi):
+    return lst[:, lo // 16 : hi // 16]
+
+
+def tile_picked_hashbiggdif_none_p_kernel(tc, x_words, x_scales, w1, gn, w2, offs, n1, n2, n3, out):
+    nc = tc.nc
+    with ExitStack() as ctx:
+        keep = ctx.enter_context(tc.tile_pool(name="keep", bufs=1))
+        psum = ctx.enter_context(tc.psum_pool(name="psum", bufs=1))
+
+        offs_t = keep.tile([P, S // 16], U16, name="offs_t")
+        n1_t = keep.tile([P, S // 16], U16, name="n1_t")
+        n2_t = keep.tile([P, S // 16], U16, name="n2_t")
+        n3_t = keep.tile([P, S // 16], U16, name="n3_t")
+        table_words = keep.tile([P, T], I32, name="table_words", align_bytes=64)
+        table_scales = keep.tile([P, T], U8, name="table_scales", align_bytes=64)
+        x_codes = keep.tile([P, S], U32, name="x_codes", align_bytes=64)
+        picked_scales = keep.tile([P, S], U8, name="picked_scales", align_bytes=64)
+        x_plane = keep.tile([P, S], U8, name="x_plane", align_bytes=64)
+        w1_raw = keep.tile([P, PACK, H], F32, name="w1_raw", tag="w_raw", align_bytes=64)
+        gain = keep.tile([P, PACK], F32, name="gain")
+        gain_sign = keep.tile([P, PACK], F32, name="gain_sign")
+        gain_abs = keep.tile([P, PACK], F32, name="gain_abs")
+        preload = keep.tile([P, 2], F32, name="preload")
+
+        nc.gpsimd.memset(table_scales[:].bitcast(I32), 0)
+        nc.vector.memset(preload[:, 0:1], 0.0)
+        nc.vector.memset(x_plane[:].bitcast(I32), 0)
+
+        nc.sync.dma_start(offs_t[:], offs)
+        nc.scalar.dma_start(table_scales[0:P:8, :].bitcast(I32), x_scales[0].bitcast(I32))
+        nc.sync.dma_start(w1_raw[:], w1.rearrange("(p j) c -> p j c", j=PACK))
+        nc.sync.dma_start(n1_t[:], n1)
+        nc.sync.dma_start(n2_t[:], n2)
+        nc.sync.dma_start(n3_t[:], n3)
+        nc.sync.dma_start(table_words[:], x_words[0].rearrange("p n t -> p (n t)").bitcast(I32))
+        nc.gpsimd.dma_start(gain[:], gn.rearrange("(p j) o -> p (j o)", j=PACK))
+        nc.scalar.activation(preload[:, 1:2], preload[:, 0:1], ACT.Sigmoid)
+
+        nc.gpsimd.tensor_scalar(gain_sign[:], gain[:], 0.0, 2.0, ALU.is_ge, ALU.mult)
+        nc.gpsimd.tensor_scalar(gain_sign[:], gain_sign[:], 1.0, -1.0, ALU.mult, ALU.add)
+        nc.gpsimd.tensor_tensor(gain_abs[:], gain[:], gain_sign[:], ALU.mult)
+
+        nc.vector.tensor_copy(picked_scales[:], table_scales[:].indirect(offs_t[:]))
+        for b in range(4):
+            nc.scalar.dma_start(x_plane[b:P:32, :].bitcast(I32), picked_scales[8 * b : P : 32, :].bitcast(I32))
+
+        w1_bf = keep.tile([P, PACK, P, PACK], BF16, name="w1_bf", align_bytes=64)
+        w1_codes = keep.tile([P, H], U32, name="w1_codes", tag="w1_codes", align_bytes=64)
+        w1_plane = keep.tile([P, H], U8, name="w1_plane", align_bytes=64)
+        w2_codes = keep.tile([P, N], U32, name="w2_codes", align_bytes=64)
+        w2_plane = keep.tile([P, N], U8, name="w2_plane", align_bytes=64)
+
+        nc.vector.tensor_copy(w1_bf[:].rearrange("p t m j -> p m t j"), w1_raw[:].rearrange("p j (m t) -> p m t j", t=PACK))
+        w2_raw = keep.tile([P, PACK, N], F32, name="w2_raw", tag="w_raw", align_bytes=64)
+        nc.sync.dma_start(w2_raw[:], w2.rearrange("(p j) c -> p j c", j=PACK))
+        nc.vector.quantize_mx(w1_codes[:].bitcast(FP8X4), w1_plane[:], w1_bf[:].rearrange("p t m j -> p (t m j)"))
+
+        for lo in (0, HALF):
+            nc.vector.tensor_copy(x_codes[:, lo : lo + HALF], table_words[:].bitcast(U32).indirect(entries(offs_t, lo, lo + HALF)))
+
+        def product(acc, codes, plane, t, rhs_codes, rhs_plane, lo, hi):
+            nc.tensor.matmul_mx(
+                out=acc[:, lo:hi],
+                lhsT=codes[:, t * P : (t + 1) * P].bitcast(FP8X4),
+                lhsT_scale=plane[:, t * P : (t + 1) * P],
+                rhs=rhs_codes[:, lo:hi].bitcast(FP8X4),
+                rhs_scale=rhs_plane[:, lo:hi],
+                start=True,
+                stop=True,
+            )
+
+        y_acc = [psum.tile([P, S], F32, name=f"y_acc{t}") for t in range(PACK)]
+        y_win = [keep.tile([P, S], F32, name=f"y_win{t}", align_bytes=64) for t in range(PACK)]
+        for t in range(PACK):
+            for lo, hi in ((0, HALF), (HALF, S)) if t == 0 else ((0, S),):
+                product(y_acc[t], w1_codes, w1_plane, t, x_codes, x_plane, lo, hi)
+                nc.scalar.activation(y_win[t][:, lo:hi], y_acc[t][:, lo:hi], ACT.Copy, scale=gain_abs[:, t : t + 1])
+
+        w2_bf = keep.tile([P, PACK, P, PACK], BF16, name="w2_bf", tag="w1_codes", align_bytes=64)
+        nc.scalar.copy(w2_bf[:].rearrange("p t m j -> p m t j"), w2_raw[:].rearrange("p j (m t) -> p m t j", t=PACK))
+
+        h_acc = [psum.tile([P, S], F32, name=f"h_acc{t}") for t in range(PACK)]
+        h_win = [keep.tile([P, 2 * S], F32, name=f"h_win{t}", align_bytes=64) for t in range(PACK)]
+        for t in range(PACK):
+            nc.gpsimd.memset(h_win[t][:, S:], 0.0)
+        z_codes = keep.tile([P, S], U32, name="z_codes", align_bytes=64)
+        z_plane = keep.tile([P, S], U8, name="z_plane", align_bytes=64)
+        z_rows = []
+        for i, (lo, hi) in enumerate(FETCH_PIECES):
+            w = hi - lo
+            larger = keep.tile([P, PACK, w], BF16, name=f"larger{i}", align_bytes=64)
+            z_rows.append(keep.tile([P, PACK, w], BF16, name=f"z_rows{i}", align_bytes=64))
+            if i == 0:
+                fetched = [keep.tile([P, w], F32, name=f"fetched{t}", tag=f"fetched{t}", align_bytes=64)[:] for t in range(PACK)]
+            else:
+                late = keep.tile([P, PACK, w], F32, name="fetched_late", tag=f"fetched{PACK - 1}", align_bytes=64)
+                fetched = [late[:, t, :] for t in range(PACK)]
+            for t in range(PACK):
+                nc.vector.tensor_copy(fetched[t], y_win[t][:].indirect(entries(n1_t, lo, hi)))
+            for t in range(PACK):
+                nc.vector.scalar_tensor_tensor(larger[:, t, :], y_acc[t][:, lo:hi], gain_abs[:, t : t + 1], fetched[t], ALU.mult, ALU.max)
+            for t in range(PACK):
+                nc.vector.tensor_scalar(z_rows[i][:, t, :], larger[:, t, :], gain_sign[:, t : t + 1], None, ALU.mult)
+
+        nc.vector.quantize_mx(w2_codes[:].bitcast(FP8X4), w2_plane[:], w2_bf[:].rearrange("p t m j -> p (t m j)"))
+        for i, (lo, hi) in enumerate(Z_PIECES):
+            last = i == len(Z_PIECES) - 1
+            z_bf = keep.tile([P, (hi - lo) * PACK], BF16, name=f"z_bf{i}", align_bytes=64)
+            woven = z_bf[:].rearrange("p (c i t) -> p c t i", i=4, t=PACK)
+            if last:
+                nc.vector.tensor_copy(woven, z_rows[1][:].rearrange("p t (c i) -> p c t i", i=4))
+            else:
+                nc.scalar.copy(woven, z_rows[0][:, :, lo:hi].rearrange("p t (c i) -> p c t i", i=4))
+            nc.vector.quantize_mx(z_codes[:, lo:hi].bitcast(FP8X4), z_plane[:, lo:hi], z_bf[:])
+            product(h_acc[0], w2_codes, w2_plane, 0, z_codes, z_plane, lo, hi)
+
+        out_rows = out.rearrange("(p t) c -> p t c", t=PACK)
+        for t in range(PACK):
+            if t > 0:
+                product(h_acc[t], w2_codes, w2_plane, t, z_codes, z_plane, 0, S)
+            nc.scalar.copy(h_win[t][:, 0:S], h_acc[t][:])
+            other = keep.tile([P, S], F32, name=f"other{t}", align_bytes=64)
+            gate = keep.tile([P, S], F32, name=f"gate{t}", align_bytes=64)
+            diff = keep.tile([P, S], F32, name=f"diff{t}", align_bytes=64)
+            res = keep.tile([P, S], F32, name=f"res{t}", align_bytes=64)
+            nc.vector.tensor_copy(other[:], h_win[t][:].indirect(n2_t[:]))
+            nc.scalar.activation(gate[:], h_win[t][:].indirect(n3_t[:]), ACT.Sigmoid)
+            for lo, hi in ((0, HALF), (HALF, S)) if t == PACK - 1 else ((0, S),):
+                nc.vector.tensor_tensor(diff[:, lo:hi], h_acc[t][:, lo:hi], other[:, lo:hi], ALU.subtract)
+                nc.vector.tensor_tensor(res[:, lo:hi], diff[:, lo:hi], gate[:, lo:hi], ALU.mult)
+                nc.sync.dma_start(out_rows[:, t, lo:hi], res[:, lo:hi])

@@ -40,25 +40,27 @@ def tile_picked_hashbiggdif_none_p_kernel(tc, x_words, x_scales, w1, gn, w2, off
         table_scales = keep.tile([P, T], U8, name="table_scales", align_bytes=64)
         x_codes = keep.tile([P, S], U32, name="x_codes", align_bytes=64)
         picked_scales = keep.tile([P, S], U8, name="picked_scales", align_bytes=64)
-        x_plane = keep.tile([P, S], U8, name="x_plane", align_bytes=64)
+        x_plane = keep.tile([P, S], U8, name="x_plane", tag="x_plane", align_bytes=64)
         w1_raw = keep.tile([P, PACK, H], F32, name="w1_raw", tag="w_raw", align_bytes=64)
         gain = keep.tile([P, PACK], F32, name="gain")
         gain_sign = keep.tile([P, PACK], F32, name="gain_sign")
         gain_abs = keep.tile([P, PACK], F32, name="gain_abs")
+        gain_zero = keep.tile([P, 1], F32, name="gain_zero")
         preload = keep.tile([P, 2], F32, name="preload")
 
         nc.gpsimd.memset(table_scales[:].bitcast(I32), 0)
         nc.vector.memset(preload[:, 0:1], 0.0)
+        nc.vector.memset(gain_zero[:], 0.0)
         nc.vector.memset(x_plane[:].bitcast(I32), 0)
 
         nc.sync.dma_start(offs_t[:], offs)
-        nc.scalar.dma_start(table_scales[0:P:8, :].bitcast(I32), x_scales[0].bitcast(I32))
-        nc.sync.dma_start(w1_raw[:], w1.rearrange("(p j) c -> p j c", j=PACK))
+        nc.sync.dma_start(table_scales[0:P:8, :].bitcast(I32), x_scales[0].bitcast(I32))
         nc.sync.dma_start(n1_t[:], n1)
         nc.sync.dma_start(n2_t[:], n2)
         nc.sync.dma_start(n3_t[:], n3)
+        nc.sync.dma_start(gain[:], gn.rearrange("(p j) o -> p (j o)", j=PACK))
+        nc.sync.dma_start(w1_raw[:], w1.rearrange("(p j) c -> p j c", j=PACK))
         nc.sync.dma_start(table_words[:], x_words[0].rearrange("p n t -> p (n t)").bitcast(I32))
-        nc.gpsimd.dma_start(gain[:], gn.rearrange("(p j) o -> p (j o)", j=PACK))
         nc.scalar.activation(preload[:, 1:2], preload[:, 0:1], ACT.Sigmoid)
 
         nc.gpsimd.tensor_scalar(gain_sign[:], gain[:], 0.0, 2.0, ALU.is_ge, ALU.mult)
@@ -70,14 +72,16 @@ def tile_picked_hashbiggdif_none_p_kernel(tc, x_words, x_scales, w1, gn, w2, off
             nc.scalar.dma_start(x_plane[b:P:32, :].bitcast(I32), picked_scales[8 * b : P : 32, :].bitcast(I32))
 
         w1_bf = keep.tile([P, PACK, P, PACK], BF16, name="w1_bf", align_bytes=64)
-        w1_codes = keep.tile([P, H], U32, name="w1_codes", tag="w1_codes", align_bytes=64)
+        w1_codes = keep.tile([P, H], U32, name="w1_codes", align_bytes=64)
         w1_plane = keep.tile([P, H], U8, name="w1_plane", align_bytes=64)
-        w2_codes = keep.tile([P, N], U32, name="w2_codes", align_bytes=64)
         w2_plane = keep.tile([P, N], U8, name="w2_plane", align_bytes=64)
 
         nc.vector.tensor_copy(w1_bf[:].rearrange("p t m j -> p m t j"), w1_raw[:].rearrange("p j (m t) -> p m t j", t=PACK))
         w2_raw = keep.tile([P, PACK, N], F32, name="w2_raw", tag="w_raw", align_bytes=64)
-        nc.sync.dma_start(w2_raw[:], w2.rearrange("(p j) c -> p j c", j=PACK))
+        for j in (0, 2):
+            nc.sync.dma_start(w2_raw[:, j : j + 2, :], w2.rearrange("(p j) c -> p j c", j=PACK)[:, j : j + 2, :])
+        for j in range(PACK):
+            nc.gpsimd.tensor_scalar(w2_raw[:, j, :], w2_raw[:, j, :], gain_sign[:, j : j + 1], gain_zero[:], ALU.mult, ALU.add)
         nc.vector.quantize_mx(w1_codes[:].bitcast(FP8X4), w1_plane[:], w1_bf[:].rearrange("p t m j -> p (t m j)"))
 
         for lo in (0, HALF):
@@ -95,62 +99,86 @@ def tile_picked_hashbiggdif_none_p_kernel(tc, x_words, x_scales, w1, gn, w2, off
             )
 
         y_acc = [psum.tile([P, S], F32, name=f"y_acc{t}") for t in range(PACK)]
-        y_win = [keep.tile([P, S], F32, name=f"y_win{t}", align_bytes=64) for t in range(PACK)]
+        y_win = [keep.tile([P, S], F32, name=f"y_win{t}", tag=f"y_win{t}", align_bytes=64) for t in range(PACK)]
         for t in range(PACK):
             for lo, hi in ((0, HALF), (HALF, S)) if t == 0 else ((0, S),):
                 product(y_acc[t], w1_codes, w1_plane, t, x_codes, x_plane, lo, hi)
                 nc.scalar.activation(y_win[t][:, lo:hi], y_acc[t][:, lo:hi], ACT.Copy, scale=gain_abs[:, t : t + 1])
 
-        w2_bf = keep.tile([P, PACK, P, PACK], BF16, name="w2_bf", tag="w1_codes", align_bytes=64)
-        nc.scalar.copy(w2_bf[:].rearrange("p t m j -> p m t j"), w2_raw[:].rearrange("p j (m t) -> p m t j", t=PACK))
+        w2_bf = keep.tile([P, PACK, P, PACK], BF16, name="w2_bf", tag="x_plane", align_bytes=64)
+        for t in range(PACK):
+            nc.scalar.copy(
+                w2_bf[:, t].rearrange("p (a c i) j -> p a c j i", c=2, i=4),
+                w2_raw[:].rearrange("p j (a t c i) -> p t a c j i", t=PACK, c=2, i=4)[:, t],
+            )
 
         h_acc = [psum.tile([P, S], F32, name=f"h_acc{t}") for t in range(PACK)]
         h_win = [keep.tile([P, 2 * S], F32, name=f"h_win{t}", align_bytes=64) for t in range(PACK)]
         for t in range(PACK):
             nc.gpsimd.memset(h_win[t][:, S:], 0.0)
-        z_codes = keep.tile([P, S], U32, name="z_codes", align_bytes=64)
         z_plane = keep.tile([P, S], U8, name="z_plane", align_bytes=64)
+        fetched = [
+            [keep.tile([P, hi - lo], F32, name=f"fetched{i}_{t}", tag=f"fetched{i}_{t}", align_bytes=64) for t in range(PACK)]
+            for i, (lo, hi) in enumerate(FETCH_PIECES)
+        ]
+        for t in range(PACK):
+            for i, (lo, hi) in enumerate(FETCH_PIECES):
+                nc.vector.tensor_copy(fetched[i][t][:], y_win[t][:].indirect(entries(n1_t, lo, hi)))
         z_rows = []
         for i, (lo, hi) in enumerate(FETCH_PIECES):
-            w = hi - lo
-            larger = keep.tile([P, PACK, w], BF16, name=f"larger{i}", align_bytes=64)
-            z_rows.append(keep.tile([P, PACK, w], BF16, name=f"z_rows{i}", align_bytes=64))
-            if i == 0:
-                fetched = [keep.tile([P, w], F32, name=f"fetched{t}", tag=f"fetched{t}", align_bytes=64)[:] for t in range(PACK)]
-            else:
-                late = keep.tile([P, PACK, w], F32, name="fetched_late", tag=f"fetched{PACK - 1}", align_bytes=64)
-                fetched = [late[:, t, :] for t in range(PACK)]
+            tag = "z_rows" if i == 0 else f"fetched0_{PACK - 1}"
+            z_rows.append(keep.tile([P, PACK, hi - lo], BF16, name=f"z_rows{i}", tag=tag, align_bytes=64))
             for t in range(PACK):
-                nc.vector.tensor_copy(fetched[t], y_win[t][:].indirect(entries(n1_t, lo, hi)))
-            for t in range(PACK):
-                nc.vector.scalar_tensor_tensor(larger[:, t, :], y_acc[t][:, lo:hi], gain_abs[:, t : t + 1], fetched[t], ALU.mult, ALU.max)
-            for t in range(PACK):
-                nc.vector.tensor_scalar(z_rows[i][:, t, :], larger[:, t, :], gain_sign[:, t : t + 1], None, ALU.mult)
+                nc.vector.scalar_tensor_tensor(
+                    z_rows[i][:, t, :], y_acc[t][:, lo:hi], gain_abs[:, t : t + 1], fetched[i][t][:], ALU.mult, ALU.max
+                )
 
+        w2_codes = keep.tile([P, N], U32, name="w2_codes", tag=f"y_win{PACK - 1}", align_bytes=64)
         nc.vector.quantize_mx(w2_codes[:].bitcast(FP8X4), w2_plane[:], w2_bf[:].rearrange("p t m j -> p (t m j)"))
-        for i, (lo, hi) in enumerate(Z_PIECES):
-            last = i == len(Z_PIECES) - 1
-            z_bf = keep.tile([P, (hi - lo) * PACK], BF16, name=f"z_bf{i}", align_bytes=64)
-            woven = z_bf[:].rearrange("p (c i t) -> p c t i", i=4, t=PACK)
-            if last:
+        z_codes = keep.tile([P, S], U32, name="z_codes", align_bytes=64)
+        z_bf = [keep.tile([P, (hi - lo) * PACK], BF16, name=f"z_bf{i}", align_bytes=64) for i, (lo, hi) in enumerate(Z_PIECES)]
+
+        def weave(i):
+            lo, hi = Z_PIECES[i]
+            woven = z_bf[i][:].rearrange("p (c i t) -> p c t i", i=4, t=PACK)
+            if i == len(Z_PIECES) - 1:
                 nc.vector.tensor_copy(woven, z_rows[1][:].rearrange("p t (c i) -> p c t i", i=4))
             else:
                 nc.scalar.copy(woven, z_rows[0][:, :, lo:hi].rearrange("p t (c i) -> p c t i", i=4))
-            nc.vector.quantize_mx(z_codes[:, lo:hi].bitcast(FP8X4), z_plane[:, lo:hi], z_bf[:])
+
+        def quantise(i):
+            lo, hi = Z_PIECES[i]
+            nc.vector.quantize_mx(z_codes[:, lo:hi].bitcast(FP8X4), z_plane[:, lo:hi], z_bf[i][:])
             product(h_acc[0], w2_codes, w2_plane, 0, z_codes, z_plane, lo, hi)
 
-        out_rows = out.rearrange("(p t) c -> p t c", t=PACK)
+        weave(0)
+        weave(1)
+        quantise(0)
+        nc.scalar.copy(h_win[0][:, 0:HALF], h_acc[0][:, 0:HALF])
+        weave(2)
+        quantise(1)
+        quantise(2)
+        nc.scalar.copy(h_win[0][:, HALF:S], h_acc[0][:, HALF:S])
+
+        out_rows = out.rearrange("(a t c) n -> t a c n", t=PACK, c=8)
         for t in range(PACK):
-            if t > 0:
-                product(h_acc[t], w2_codes, w2_plane, t, z_codes, z_plane, 0, S)
-            nc.scalar.copy(h_win[t][:, 0:S], h_acc[t][:])
+            if t + 1 < PACK:
+                product(h_acc[t + 1], w2_codes, w2_plane, t + 1, z_codes, z_plane, 0, S)
+                nc.scalar.copy(h_win[t + 1][:, 0:S], h_acc[t + 1][:])
             other = keep.tile([P, S], F32, name=f"other{t}", align_bytes=64)
             gate = keep.tile([P, S], F32, name=f"gate{t}", align_bytes=64)
-            diff = keep.tile([P, S], F32, name=f"diff{t}", align_bytes=64)
             res = keep.tile([P, S], F32, name=f"res{t}", align_bytes=64)
             nc.vector.tensor_copy(other[:], h_win[t][:].indirect(n2_t[:]))
             nc.scalar.activation(gate[:], h_win[t][:].indirect(n3_t[:]), ACT.Sigmoid)
-            for lo, hi in ((0, HALF), (HALF, S)) if t == PACK - 1 else ((0, S),):
-                nc.vector.tensor_tensor(diff[:, lo:hi], h_acc[t][:, lo:hi], other[:, lo:hi], ALU.subtract)
-                nc.vector.tensor_tensor(res[:, lo:hi], diff[:, lo:hi], gate[:, lo:hi], ALU.mult)
-                nc.sync.dma_start(out_rows[:, t, lo:hi], res[:, lo:hi])
+            if t + 1 < PACK:
+                diff = h_win[t][:, S:]
+                nc.vector.tensor_tensor(diff, h_acc[t][:], other[:], ALU.subtract)
+                nc.gpsimd.tensor_tensor(res[:], diff, gate[:], ALU.mult)
+                nc.sync.dma_start(out_rows[t], res[:])
+            else:
+                last_diff = keep.tile([P, S], F32, name="last_diff", align_bytes=64)
+                for lo in (0, HALF):
+                    nc.vector.tensor_tensor(last_diff[:, lo : lo + HALF], h_acc[t][:, lo : lo + HALF], other[:, lo : lo + HALF], ALU.subtract)
+                for lo in (0, HALF):
+                    nc.vector.tensor_tensor(res[:, lo : lo + HALF], last_diff[:, lo : lo + HALF], gate[:, lo : lo + HALF], ALU.mult)
+                    nc.sync.dma_start(out_rows[t, :, :, lo : lo + HALF], res[:, lo : lo + HALF])

@@ -18,6 +18,7 @@ ACT = mybir.ActivationFunctionType
 P = 128
 PACK = 4
 HALF = S // 2
+VECTOR_SHARE = 88
 FETCH_PIECES = ((0, 384), (384, 512))
 Z_PIECES = ((0, 256), (256, 384), (384, 512))
 
@@ -37,11 +38,11 @@ def tile_picked_hashbiggdif_none_p_kernel(tc, x_words, x_scales, w1, gn, w2, off
         n2_t = keep.tile([P, S // 16], U16, name="n2_t")
         n3_t = keep.tile([P, S // 16], U16, name="n3_t")
         table_words = keep.tile([P, T], I32, name="table_words", align_bytes=64)
-        table_scales = keep.tile([P, T], U8, name="table_scales", align_bytes=64)
+        table_scales = keep.tile([P, T], U8, name="table_scales", tag="table_scales", align_bytes=64)
         x_codes = keep.tile([P, S], U32, name="x_codes", align_bytes=64)
         picked_scales = keep.tile([P, S], U8, name="picked_scales", align_bytes=64)
         x_plane = keep.tile([P, S], U8, name="x_plane", tag="x_plane", align_bytes=64)
-        w1_raw = keep.tile([P, PACK, H], F32, name="w1_raw", tag="w_raw", align_bytes=64)
+        w1_pairs = [keep.tile([P, 2, H], F32, name=f"w1_pair{u}", align_bytes=64) for u in range(2)]
         gain = keep.tile([P, PACK], F32, name="gain")
         gain_sign = keep.tile([P, PACK], F32, name="gain_sign")
         gain_abs = keep.tile([P, PACK], F32, name="gain_abs")
@@ -59,8 +60,9 @@ def tile_picked_hashbiggdif_none_p_kernel(tc, x_words, x_scales, w1, gn, w2, off
         nc.sync.dma_start(n2_t[:], n2)
         nc.sync.dma_start(n3_t[:], n3)
         nc.sync.dma_start(gain[:], gn.rearrange("(p j) o -> p (j o)", j=PACK))
-        nc.sync.dma_start(w1_raw[:], w1.rearrange("(p j) c -> p j c", j=PACK))
         nc.sync.dma_start(table_words[:], x_words[0].rearrange("p n t -> p (n t)").bitcast(I32))
+        for u in range(2):
+            nc.sync.dma_start(w1_pairs[u][:], w1.rearrange("(p j) c -> p j c", j=PACK)[:, 2 * u : 2 * u + 2, :])
         nc.scalar.activation(preload[:, 1:2], preload[:, 0:1], ACT.Sigmoid)
 
         nc.gpsimd.tensor_scalar(gain_sign[:], gain[:], 0.0, 2.0, ALU.is_ge, ALU.mult)
@@ -71,21 +73,28 @@ def tile_picked_hashbiggdif_none_p_kernel(tc, x_words, x_scales, w1, gn, w2, off
         for b in range(4):
             nc.scalar.dma_start(x_plane[b:P:32, :].bitcast(I32), picked_scales[8 * b : P : 32, :].bitcast(I32))
 
-        w1_bf = keep.tile([P, PACK, P, PACK], BF16, name="w1_bf", align_bytes=64)
+        w1_bf = keep.tile([P, PACK, P, PACK], BF16, name="w1_bf", tag="w1_bf", align_bytes=64)
         w1_codes = keep.tile([P, H], U32, name="w1_codes", align_bytes=64)
         w1_plane = keep.tile([P, H], U8, name="w1_plane", align_bytes=64)
         w2_plane = keep.tile([P, N], U8, name="w2_plane", align_bytes=64)
 
-        nc.vector.tensor_copy(w1_bf[:].rearrange("p t m j -> p m t j"), w1_raw[:].rearrange("p j (m t) -> p m t j", t=PACK))
-        w2_raw = keep.tile([P, PACK, N], F32, name="w2_raw", tag="w_raw", align_bytes=64)
+        w2_raw = keep.tile([P, PACK, N], F32, name="w2_raw", tag="table_scales", align_bytes=64)
         for j in (0, 2):
-            nc.sync.dma_start(w2_raw[:, j : j + 2, :], w2.rearrange("(p j) c -> p j c", j=PACK)[:, j : j + 2, :])
-        for j in range(PACK):
-            nc.gpsimd.tensor_scalar(w2_raw[:, j, :], w2_raw[:, j, :], gain_sign[:, j : j + 1], gain_zero[:], ALU.mult, ALU.add)
-        nc.vector.quantize_mx(w1_codes[:].bitcast(FP8X4), w1_plane[:], w1_bf[:].rearrange("p t m j -> p (t m j)"))
+            nc.scalar.dma_start(w2_raw[:, j : j + 2, :], w2.rearrange("(p j) c -> p j c", j=PACK)[:, j : j + 2, :])
 
-        for lo in (0, HALF):
-            nc.vector.tensor_copy(x_codes[:, lo : lo + HALF], table_words[:].bitcast(U32).indirect(entries(offs_t, lo, lo + HALF)))
+        nc.vector.tensor_copy(x_codes[:], table_words[:].bitcast(U32).indirect(offs_t[:]))
+        w1_dealt = w1_bf[:].rearrange("p t m j -> p m t j")
+        w1_rows = [pair[:].rearrange("p j (m t) -> p m t j", t=PACK) for pair in w1_pairs]
+        nc.vector.tensor_copy(w1_dealt[:, :, :, 0:2], w1_rows[0])
+        nc.vector.tensor_copy(w1_dealt[:, :VECTOR_SHARE, :, 2:4], w1_rows[1][:, :VECTOR_SHARE])
+        nc.scalar.copy(w1_dealt[:, VECTOR_SHARE:, :, 2:4], w1_rows[1][:, VECTOR_SHARE:])
+        for t in range(PACK):
+            cols = slice(t * P, (t + 1) * P)
+            nc.vector.quantize_mx(w1_codes[:, cols].bitcast(FP8X4), w1_plane[:, cols], w1_bf[:, t].rearrange("p m j -> p (m j)"))
+        w2_signed = keep.tile([P, PACK, N], F32, name="w2_signed", tag="w1_bf", align_bytes=64)
+        for j in range(PACK):
+            engine = nc.vector if j < 2 else nc.gpsimd
+            engine.tensor_scalar(w2_signed[:, j, :], w2_raw[:, j, :], gain_sign[:, j : j + 1], gain_zero[:], ALU.mult, ALU.add)
 
         def product(acc, codes, plane, t, rhs_codes, rhs_plane, lo, hi):
             nc.tensor.matmul_mx(
@@ -101,15 +110,14 @@ def tile_picked_hashbiggdif_none_p_kernel(tc, x_words, x_scales, w1, gn, w2, off
         y_acc = [psum.tile([P, S], F32, name=f"y_acc{t}") for t in range(PACK)]
         y_win = [keep.tile([P, S], F32, name=f"y_win{t}", tag=f"y_win{t}", align_bytes=64) for t in range(PACK)]
         for t in range(PACK):
-            for lo, hi in ((0, HALF), (HALF, S)) if t == 0 else ((0, S),):
-                product(y_acc[t], w1_codes, w1_plane, t, x_codes, x_plane, lo, hi)
-                nc.scalar.activation(y_win[t][:, lo:hi], y_acc[t][:, lo:hi], ACT.Copy, scale=gain_abs[:, t : t + 1])
+            product(y_acc[t], w1_codes, w1_plane, t, x_codes, x_plane, 0, S)
+            nc.scalar.activation(y_win[t][:], y_acc[t][:], ACT.Copy, scale=gain_abs[:, t : t + 1])
 
         w2_bf = keep.tile([P, PACK, P, PACK], BF16, name="w2_bf", tag="x_plane", align_bytes=64)
         for t in range(PACK):
             nc.scalar.copy(
                 w2_bf[:, t].rearrange("p (a c i) j -> p a c j i", c=2, i=4),
-                w2_raw[:].rearrange("p j (a t c i) -> p t a c j i", t=PACK, c=2, i=4)[:, t],
+                w2_signed[:].rearrange("p j (a t c i) -> p t a c j i", t=PACK, c=2, i=4)[:, t],
             )
 
         h_acc = [psum.tile([P, S], F32, name=f"h_acc{t}") for t in range(PACK)]

@@ -18,8 +18,7 @@ ACT = mybir.ActivationFunctionType
 P = 128
 PACK = 4
 HALF = S // 2
-VECTOR_SHARE = 88
-FETCH_PIECES = ((0, 384), (384, 512))
+FETCH_PIECES = ((0, 256), (256, 512))
 Z_PIECES = ((0, 256), (256, 384), (384, 512))
 
 
@@ -46,12 +45,10 @@ def tile_picked_hashbiggdif_none_p_kernel(tc, x_words, x_scales, w1, gn, w2, off
         gain = keep.tile([P, PACK], F32, name="gain")
         gain_sign = keep.tile([P, PACK], F32, name="gain_sign")
         gain_abs = keep.tile([P, PACK], F32, name="gain_abs")
-        gain_zero = keep.tile([P, 1], F32, name="gain_zero")
         preload = keep.tile([P, 2], F32, name="preload")
 
         nc.gpsimd.memset(table_scales[:].bitcast(I32), 0)
         nc.vector.memset(preload[:, 0:1], 0.0)
-        nc.vector.memset(gain_zero[:], 0.0)
         nc.vector.memset(x_plane[:].bitcast(I32), 0)
 
         nc.sync.dma_start(offs_t[:], offs)
@@ -86,15 +83,16 @@ def tile_picked_hashbiggdif_none_p_kernel(tc, x_words, x_scales, w1, gn, w2, off
         w1_dealt = w1_bf[:].rearrange("p t m j -> p m t j")
         w1_rows = [pair[:].rearrange("p j (m t) -> p m t j", t=PACK) for pair in w1_pairs]
         nc.vector.tensor_copy(w1_dealt[:, :, :, 0:2], w1_rows[0])
-        nc.vector.tensor_copy(w1_dealt[:, :VECTOR_SHARE, :, 2:4], w1_rows[1][:, :VECTOR_SHARE])
-        nc.scalar.copy(w1_dealt[:, VECTOR_SHARE:, :, 2:4], w1_rows[1][:, VECTOR_SHARE:])
+        nc.vector.tensor_copy(w1_dealt[:, :, 0, 2:4], w1_rows[1][:, :, 0])
+        nc.scalar.copy(w1_dealt[:, :, 1:3, 2:4], w1_rows[1][:, :, 1:3])
+        nc.vector.tensor_copy(w1_dealt[:, :, 3, 2:4], w1_rows[1][:, :, 3])
         for t in range(PACK):
             cols = slice(t * P, (t + 1) * P)
             nc.vector.quantize_mx(w1_codes[:, cols].bitcast(FP8X4), w1_plane[:, cols], w1_bf[:, t].rearrange("p m j -> p (m j)"))
         w2_signed = keep.tile([P, PACK, N], F32, name="w2_signed", tag="w1_bf", align_bytes=64)
         for j in range(PACK):
             engine = nc.vector if j < 2 else nc.gpsimd
-            engine.tensor_scalar(w2_signed[:, j, :], w2_raw[:, j, :], gain_sign[:, j : j + 1], gain_zero[:], ALU.mult, ALU.add)
+            engine.tensor_scalar(w2_signed[:, j, :], w2_raw[:, j, :], gain_sign[:, j : j + 1], 0.0, ALU.mult, ALU.add)
 
         def product(acc, codes, plane, t, rhs_codes, rhs_plane, lo, hi):
             nc.tensor.matmul_mx(
@@ -132,61 +130,83 @@ def tile_picked_hashbiggdif_none_p_kernel(tc, x_words, x_scales, w1, gn, w2, off
         for t in range(PACK):
             for i, (lo, hi) in enumerate(FETCH_PIECES):
                 nc.vector.tensor_copy(fetched[i][t][:], y_win[t][:].indirect(entries(n1_t, lo, hi)))
-        z_rows = []
-        for i, (lo, hi) in enumerate(FETCH_PIECES):
-            tag = "z_rows" if i == 0 else f"fetched0_{PACK - 1}"
-            z_rows.append(keep.tile([P, PACK, hi - lo], BF16, name=f"z_rows{i}", tag=tag, align_bytes=64))
+        z_early = keep.tile([P, PACK, HALF], BF16, name="z_early", align_bytes=64)
+        z_late = keep.tile([P, 2, PACK, HALF // 2], BF16, name="z_late", tag=f"fetched0_{PACK - 1}", align_bytes=64)
+        z_rows = [z_early[:], z_late[:, 0], z_late[:, 1]]
+
+        def larger(i):
+            lo, hi = Z_PIECES[i]
             for t in range(PACK):
                 nc.vector.scalar_tensor_tensor(
-                    z_rows[i][:, t, :], y_acc[t][:, lo:hi], gain_abs[:, t : t + 1], fetched[i][t][:], ALU.mult, ALU.max
+                    z_rows[i][:, t, :],
+                    y_acc[t][:, lo:hi],
+                    gain_abs[:, t : t + 1],
+                    fetched[lo // HALF][t][:, lo % HALF : lo % HALF + hi - lo],
+                    ALU.mult,
+                    ALU.max,
                 )
 
         w2_codes = keep.tile([P, N], U32, name="w2_codes", tag=f"y_win{PACK - 1}", align_bytes=64)
-        nc.vector.quantize_mx(w2_codes[:].bitcast(FP8X4), w2_plane[:], w2_bf[:].rearrange("p t m j -> p (t m j)"))
         z_codes = keep.tile([P, S], U32, name="z_codes", align_bytes=64)
         z_bf = [keep.tile([P, (hi - lo) * PACK], BF16, name=f"z_bf{i}", align_bytes=64) for i, (lo, hi) in enumerate(Z_PIECES)]
 
         def weave(i):
-            lo, hi = Z_PIECES[i]
             woven = z_bf[i][:].rearrange("p (c i t) -> p c t i", i=4, t=PACK)
+            rows = z_rows[i].rearrange("p t (c i) -> p c t i", i=4)
             if i == len(Z_PIECES) - 1:
-                nc.vector.tensor_copy(woven, z_rows[1][:].rearrange("p t (c i) -> p c t i", i=4))
+                nc.vector.tensor_copy(woven, rows)
             else:
-                nc.scalar.copy(woven, z_rows[0][:, :, lo:hi].rearrange("p t (c i) -> p c t i", i=4))
+                nc.scalar.copy(woven, rows)
 
         def quantise(i):
             lo, hi = Z_PIECES[i]
             nc.vector.quantize_mx(z_codes[:, lo:hi].bitcast(FP8X4), z_plane[:, lo:hi], z_bf[i][:])
             product(h_acc[0], w2_codes, w2_plane, 0, z_codes, z_plane, lo, hi)
 
+        def h_half(t, lo):
+            if t > 0:
+                product(h_acc[t], w2_codes, w2_plane, t, z_codes, z_plane, lo, lo + HALF)
+            nc.scalar.copy(h_win[t][:, lo : lo + HALF], h_acc[t][:, lo : lo + HALF])
+
+        larger(0)
         weave(0)
+        larger(1)
         weave(1)
+        nc.vector.quantize_mx(w2_codes[:].bitcast(FP8X4), w2_plane[:], w2_bf[:].rearrange("p t m j -> p (t m j)"))
         quantise(0)
-        nc.scalar.copy(h_win[0][:, 0:HALF], h_acc[0][:, 0:HALF])
+        h_half(0, 0)
+        larger(2)
         weave(2)
         quantise(1)
         quantise(2)
-        nc.scalar.copy(h_win[0][:, HALF:S], h_acc[0][:, HALF:S])
+        h_half(0, HALF)
+        for t in range(1, PACK):
+            h_half(t, 0)
+        for t in range(1, PACK - 1):
+            h_half(t, HALF)
 
         out_rows = out.rearrange("(a t c) n -> t a c n", t=PACK, c=8)
+        halves = (slice(0, HALF), slice(HALF, S))
+        other = [keep.tile([P, S], F32, name=f"other{t}", align_bytes=64) for t in range(PACK)]
+        gate = [keep.tile([P, S], F32, name=f"gate{t}", align_bytes=64) for t in range(PACK)]
+        res = [keep.tile([P, S], F32, name=f"res{t}", align_bytes=64) for t in range(PACK)]
+        diff_first = keep.tile([P, S], F32, name="diff_first", align_bytes=64)
+        diff_last = keep.tile([P, S], F32, name="diff_last", align_bytes=64)
+        diff = [diff_first[:], h_win[0][:, S:], h_win[1][:, S:], diff_last[:]]
         for t in range(PACK):
-            if t + 1 < PACK:
-                product(h_acc[t + 1], w2_codes, w2_plane, t + 1, z_codes, z_plane, 0, S)
-                nc.scalar.copy(h_win[t + 1][:, 0:S], h_acc[t + 1][:])
-            other = keep.tile([P, S], F32, name=f"other{t}", align_bytes=64)
-            gate = keep.tile([P, S], F32, name=f"gate{t}", align_bytes=64)
-            res = keep.tile([P, S], F32, name=f"res{t}", align_bytes=64)
-            nc.vector.tensor_copy(other[:], h_win[t][:].indirect(n2_t[:]))
-            nc.scalar.activation(gate[:], h_win[t][:].indirect(n3_t[:]), ACT.Sigmoid)
-            if t + 1 < PACK:
-                diff = h_win[t][:, S:]
-                nc.vector.tensor_tensor(diff, h_acc[t][:], other[:], ALU.subtract)
-                nc.gpsimd.tensor_tensor(res[:], diff, gate[:], ALU.mult)
-                nc.sync.dma_start(out_rows[t], res[:])
-            else:
-                last_diff = keep.tile([P, S], F32, name="last_diff", align_bytes=64)
-                for lo in (0, HALF):
-                    nc.vector.tensor_tensor(last_diff[:, lo : lo + HALF], h_acc[t][:, lo : lo + HALF], other[:, lo : lo + HALF], ALU.subtract)
-                for lo in (0, HALF):
-                    nc.vector.tensor_tensor(res[:, lo : lo + HALF], last_diff[:, lo : lo + HALF], gate[:, lo : lo + HALF], ALU.mult)
-                    nc.sync.dma_start(out_rows[t, :, :, lo : lo + HALF], res[:, lo : lo + HALF])
+            nc.scalar.activation(gate[t][:], h_win[t][:].indirect(n3_t[:]), ACT.Sigmoid)
+            if t == 0:
+                h_half(PACK - 1, HALF)
+        for t in range(PACK):
+            nc.vector.tensor_copy(other[t][:], h_win[t][:].indirect(n2_t[:]))
+        nc.gpsimd.tensor_tensor(diff[0], h_win[0][:, 0:S], other[0][:], ALU.subtract)
+        for t in (1, 2):
+            nc.vector.tensor_tensor(diff[t], h_acc[t][:], other[t][:], ALU.subtract)
+        for c in halves:
+            nc.vector.tensor_tensor(diff[3][:, c], h_acc[3][:, c], other[3][:, c], ALU.subtract)
+        for t in (0, 1):
+            nc.gpsimd.tensor_tensor(res[t][:], diff[t], gate[t][:], ALU.mult)
+            nc.sync.dma_start(out_rows[t], res[t][:])
+        for t, c, engine in ((2, halves[0], nc.gpsimd), (2, halves[1], nc.vector), (3, halves[0], nc.vector), (3, halves[1], nc.vector)):
+            engine.tensor_tensor(res[t][:, c], diff[t][:, c], gate[t][:, c], ALU.mult)
+            nc.sync.dma_start(out_rows[t, :, :, c], res[t][:, c])

@@ -18,7 +18,6 @@ ACT = mybir.ActivationFunctionType
 P = 128
 PACK = 4
 HALF = S // 2
-FETCH_PIECES = ((0, 256), (256, 512))
 Z_PIECES = ((0, 256), (256, 384), (384, 512))
 
 
@@ -111,11 +110,24 @@ def tile_picked_hashbiggdif_none_p_kernel(tc, x_words, x_scales, w1, gn, w2, off
             product(y_acc[t], w1_codes, w1_plane, t, x_codes, x_plane, 0, S)
             nc.scalar.activation(y_win[t][:], y_acc[t][:], ACT.Copy, scale=gain_abs[:, t : t + 1])
 
-        w2_bf = keep.tile([P, PACK, P, PACK], BF16, name="w2_bf", tag="x_plane", align_bytes=64)
+        y_bf = keep.tile([P, PACK, S], BF16, name="y_bf", align_bytes=64)
         for t in range(PACK):
+            nc.scalar.activation(y_bf[:, t, :], y_acc[t][:], ACT.Copy, scale=gain_abs[:, t : t + 1])
+
+        w2_bf = keep.tile([P, PACK, P, PACK], BF16, name="w2_bf", tag="x_plane", align_bytes=64)
+        for t in (0, 1):
             nc.scalar.copy(
                 w2_bf[:, t].rearrange("p (a c i) j -> p a c j i", c=2, i=4),
                 w2_signed[:].rearrange("p j (a t c i) -> p t a c j i", t=PACK, c=2, i=4)[:, t],
+            )
+        for t in (2, 3):
+            nc.gpsimd.tensor_scalar(
+                w2_bf[:, t].rearrange("p (a c) j -> p a c j", c=8),
+                w2_signed[:].rearrange("p j (a t c) -> p t a c j", t=PACK, c=8)[:, t],
+                1.0,
+                0.0,
+                ALU.mult,
+                ALU.add,
             )
 
         h_acc = [psum.tile([P, S], F32, name=f"h_acc{t}") for t in range(PACK)]
@@ -123,28 +135,15 @@ def tile_picked_hashbiggdif_none_p_kernel(tc, x_words, x_scales, w1, gn, w2, off
         for t in range(PACK):
             nc.gpsimd.memset(h_win[t][:, S:], 0.0)
         z_plane = keep.tile([P, S], U8, name="z_plane", align_bytes=64)
-        fetched = [
-            [keep.tile([P, hi - lo], F32, name=f"fetched{i}_{t}", tag=f"fetched{i}_{t}", align_bytes=64) for t in range(PACK)]
-            for i, (lo, hi) in enumerate(FETCH_PIECES)
-        ]
+        fetched = keep.tile([P, PACK, S], BF16, name="fetched", align_bytes=64)
         for t in range(PACK):
-            for i, (lo, hi) in enumerate(FETCH_PIECES):
-                nc.vector.tensor_copy(fetched[i][t][:], y_win[t][:].indirect(entries(n1_t, lo, hi)))
-        z_early = keep.tile([P, PACK, HALF], BF16, name="z_early", align_bytes=64)
-        z_late = keep.tile([P, 2, PACK, HALF // 2], BF16, name="z_late", tag=f"fetched0_{PACK - 1}", align_bytes=64)
-        z_rows = [z_early[:], z_late[:, 0], z_late[:, 1]]
-
-        def larger(i):
-            lo, hi = Z_PIECES[i]
-            for t in range(PACK):
-                nc.vector.scalar_tensor_tensor(
-                    z_rows[i][:, t, :],
-                    y_acc[t][:, lo:hi],
-                    gain_abs[:, t : t + 1],
-                    fetched[lo // HALF][t][:, lo % HALF : lo % HALF + hi - lo],
-                    ALU.mult,
-                    ALU.max,
-                )
+            for lo in (0, HALF):
+                nc.vector.tensor_copy(fetched[:, t, lo : lo + HALF], y_win[t][:].indirect(entries(n1_t, lo, lo + HALF)))
+        z_halves = [keep.tile([P, PACK, HALF], BF16, name=f"z_half{u}", align_bytes=64) for u in range(2)]
+        for u in range(2):
+            c = slice(u * HALF, (u + 1) * HALF)
+            nc.vector.tensor_tensor(z_halves[u][:], fetched[:, :, c], y_bf[:, :, c], ALU.max)
+        z_rows = [z_halves[0][:], z_halves[1][:, :, 0 : HALF // 2], z_halves[1][:, :, HALF // 2 :]]
 
         w2_codes = keep.tile([P, N], U32, name="w2_codes", tag=f"y_win{PACK - 1}", align_bytes=64)
         z_codes = keep.tile([P, S], U32, name="z_codes", align_bytes=64)
@@ -164,26 +163,25 @@ def tile_picked_hashbiggdif_none_p_kernel(tc, x_words, x_scales, w1, gn, w2, off
             product(h_acc[0], w2_codes, w2_plane, 0, z_codes, z_plane, lo, hi)
 
         def h_half(t, lo):
-            if t > 0:
-                product(h_acc[t], w2_codes, w2_plane, t, z_codes, z_plane, lo, lo + HALF)
+            product(h_acc[t], w2_codes, w2_plane, t, z_codes, z_plane, lo, lo + HALF)
             nc.scalar.copy(h_win[t][:, lo : lo + HALF], h_acc[t][:, lo : lo + HALF])
 
-        larger(0)
         weave(0)
-        larger(1)
         weave(1)
         nc.vector.quantize_mx(w2_codes[:].bitcast(FP8X4), w2_plane[:], w2_bf[:].rearrange("p t m j -> p (t m j)"))
         quantise(0)
-        h_half(0, 0)
-        larger(2)
         weave(2)
         quantise(1)
         quantise(2)
-        h_half(0, HALF)
-        for t in range(1, PACK):
-            h_half(t, 0)
-        for t in range(1, PACK - 1):
-            h_half(t, HALF)
+        nc.scalar.copy(h_win[0][:, 0:S], h_acc[0][:])
+        h_half(1, 0)
+        h_half(1, HALF)
+
+        def h_whole(t):
+            product(h_acc[t], w2_codes, w2_plane, t, z_codes, z_plane, 0, S)
+            nc.scalar.copy(h_win[t][:, 0:S], h_acc[t][:])
+
+        h_whole(2)
 
         out_rows = out.rearrange("(a t c) n -> t a c n", t=PACK, c=8)
         halves = (slice(0, HALF), slice(HALF, S))
@@ -191,12 +189,13 @@ def tile_picked_hashbiggdif_none_p_kernel(tc, x_words, x_scales, w1, gn, w2, off
         gate = [keep.tile([P, S], F32, name=f"gate{t}", align_bytes=64) for t in range(PACK)]
         res = [keep.tile([P, S], F32, name=f"res{t}", align_bytes=64) for t in range(PACK)]
         diff_first = keep.tile([P, S], F32, name="diff_first", align_bytes=64)
-        diff_last = keep.tile([P, S], F32, name="diff_last", align_bytes=64)
-        diff = [diff_first[:], h_win[0][:, S:], h_win[1][:, S:], diff_last[:]]
-        for t in range(PACK):
+        diff = [diff_first[:]] + [h_win[t][:, S:] for t in range(PACK - 1)]
+        for t in range(PACK - 1):
             nc.scalar.activation(gate[t][:], h_win[t][:].indirect(n3_t[:]), ACT.Sigmoid)
             if t == 0:
-                h_half(PACK - 1, HALF)
+                h_whole(PACK - 1)
+        for c in halves:
+            nc.scalar.activation(gate[3][:, c], h_win[3][:].indirect(entries(n3_t, c.start, c.stop)), ACT.Sigmoid)
         for t in range(PACK):
             nc.vector.tensor_copy(other[t][:], h_win[t][:].indirect(n2_t[:]))
         nc.gpsimd.tensor_tensor(diff[0], h_win[0][:, 0:S], other[0][:], ALU.subtract)

from contextlib import ExitStack

import concourse.mybir as mybir

K, T, S, N, H = 512, 2048, 512, 512, 512
FLOPS = 2 * K * H * S + 2 * H * N * S

F32 = mybir.dt.float32
BF16 = mybir.dt.bfloat16
I32 = mybir.dt.int32
U32 = mybir.dt.uint32
U16 = mybir.dt.uint16
U8 = mybir.dt.uint8
FP8X4 = mybir.dt.float8_e4m3fn_x4
ALU = mybir.AluOpType
ACT = mybir.ActivationFunctionType

P = 128
PACK = 4
HALF = S // 2
Z_PIECES = ((0, 256), (256, 384), (384, 512))


def entries(lst, lo, hi):
    return lst[:, lo // 16 : hi // 16]


def tile_picked_hashbiggdif_none_p_kernel(tc, x_words, x_scales, w1, gn, w2, offs, n1, n2, n3, out):
    nc = tc.nc
    with ExitStack() as ctx:
        keep = ctx.enter_context(tc.tile_pool(name="keep", bufs=1))
        psum = ctx.enter_context(tc.psum_pool(name="psum", bufs=1))

        offs_t = keep.tile([P, S // 16], U16, name="offs_t")
        n1_t = keep.tile([P, S // 16], U16, name="n1_t")
        n2_t = keep.tile([P, S // 16], U16, name="n2_t")
        n3_t = keep.tile([P, S // 16], U16, name="n3_t")
        table_words = keep.tile([P, T], I32, name="table_words", align_bytes=64)
        table_scales = keep.tile([P, T], U8, name="table_scales", tag="table_scales", align_bytes=64)
        x_codes = keep.tile([P, S], U32, name="x_codes", align_bytes=64)
        picked_scales = keep.tile([P, S], U8, name="picked_scales", align_bytes=64)
        x_plane = keep.tile([P, S], U8, name="x_plane", tag="x_plane", align_bytes=64)
        w1_pairs = [keep.tile([P, 2, H], F32, name=f"w1_pair{u}", align_bytes=64) for u in range(2)]
        gain = keep.tile([P, PACK], F32, name="gain")
        gain_sign = keep.tile([P, PACK], F32, name="gain_sign")
        gain_abs = keep.tile([P, PACK], F32, name="gain_abs")
        preload = keep.tile([P, 2], F32, name="preload")

        nc.gpsimd.memset(table_scales[:].bitcast(I32), 0)
        nc.vector.memset(preload[:, 0:1], 0.0)
        nc.vector.memset(x_plane[:].bitcast(I32), 0)

        nc.sync.dma_start(offs_t[:], offs)
        nc.sync.dma_start(table_scales[0:P:8, :].bitcast(I32), x_scales[0].bitcast(I32))
        nc.sync.dma_start(n1_t[:], n1)
        nc.sync.dma_start(n2_t[:], n2)
        nc.sync.dma_start(n3_t[:], n3)
        nc.sync.dma_start(gain[:], gn.rearrange("(p j) o -> p (j o)", j=PACK))
        nc.sync.dma_start(table_words[:], x_words[0].rearrange("p n t -> p (n t)").bitcast(I32))
        for u in range(2):
            nc.sync.dma_start(w1_pairs[u][:], w1.rearrange("(p j) c -> p j c", j=PACK)[:, 2 * u : 2 * u + 2, :])
        nc.scalar.activation(preload[:, 1:2], preload[:, 0:1], ACT.Sigmoid)

        nc.gpsimd.tensor_scalar(gain_sign[:], gain[:], 0.0, 2.0, ALU.is_ge, ALU.mult)
        nc.gpsimd.tensor_scalar(gain_sign[:], gain_sign[:], 1.0, -1.0, ALU.mult, ALU.add)
        nc.gpsimd.tensor_tensor(gain_abs[:], gain[:], gain_sign[:], ALU.mult)

        nc.vector.tensor_copy(picked_scales[:], table_scales[:].indirect(offs_t[:]))
        for b in range(4):
            nc.scalar.dma_start(x_plane[b:P:32, :].bitcast(I32), picked_scales[8 * b : P : 32, :].bitcast(I32))

        w1_bf = keep.tile([P, PACK, P, PACK], BF16, name="w1_bf", tag="w1_bf", align_bytes=64)
        w1_codes = keep.tile([P, H], U32, name="w1_codes", align_bytes=64)
        w1_plane = keep.tile([P, H], U8, name="w1_plane", align_bytes=64)
        w2_plane = keep.tile([P, N], U8, name="w2_plane", align_bytes=64)

        w2_raw = keep.tile([P, PACK, N], F32, name="w2_raw", tag="table_scales", align_bytes=64)
        for j in (0, 2):
            nc.scalar.dma_start(w2_raw[:, j : j + 2, :], w2.rearrange("(p j) c -> p j c", j=PACK)[:, j : j + 2, :])

        nc.vector.tensor_copy(x_codes[:], table_words[:].bitcast(U32).indirect(offs_t[:]))
        w1_dealt = w1_bf[:].rearrange("p t m j -> p m t j")
        w1_rows = [pair[:].rearrange("p j (m t) -> p m t j", t=PACK) for pair in w1_pairs]
        nc.vector.tensor_copy(w1_dealt[:, :, :, 0:2], w1_rows[0])
        nc.vector.tensor_copy(w1_dealt[:, :, 0, 2:4], w1_rows[1][:, :, 0])
        nc.scalar.copy(w1_dealt[:, :, 1:3, 2:4], w1_rows[1][:, :, 1:3])
        nc.vector.tensor_copy(w1_dealt[:, :, 3, 2:4], w1_rows[1][:, :, 3])
        for t in range(PACK):
            cols = slice(t * P, (t + 1) * P)
            nc.vector.quantize_mx(w1_codes[:, cols].bitcast(FP8X4), w1_plane[:, cols], w1_bf[:, t].rearrange("p m j -> p (m j)"))
        w2_signed = keep.tile([P, PACK, N], F32, name="w2_signed", tag="w1_bf", align_bytes=64)
        for j in range(PACK):
            engine = nc.vector if j < 2 else nc.gpsimd
            engine.tensor_scalar(w2_signed[:, j, :], w2_raw[:, j, :], gain_sign[:, j : j + 1], 0.0, ALU.mult, ALU.add)

        def product(acc, codes, plane, t, rhs_codes, rhs_plane, lo, hi):
            nc.tensor.matmul_mx(
                out=acc[:, lo:hi],
                lhsT=codes[:, t * P : (t + 1) * P].bitcast(FP8X4),
                lhsT_scale=plane[:, t * P : (t + 1) * P],
                rhs=rhs_codes[:, lo:hi].bitcast(FP8X4),
                rhs_scale=rhs_plane[:, lo:hi],
                start=True,
                stop=True,
            )

        y_acc = [psum.tile([P, S], F32, name=f"y_acc{t}") for t in range(PACK)]
        y_win = [keep.tile([P, S], F32, name=f"y_win{t}", tag=f"y_win{t}", align_bytes=64) for t in range(PACK)]
        for t in range(PACK):
            product(y_acc[t], w1_codes, w1_plane, t, x_codes, x_plane, 0, S)
            nc.scalar.activation(y_win[t][:], y_acc[t][:], ACT.Copy, scale=gain_abs[:, t : t + 1])

        y_bf = keep.tile([P, PACK, S], BF16, name="y_bf", align_bytes=64)
        for t in range(PACK):
            nc.scalar.activation(y_bf[:, t, :], y_acc[t][:], ACT.Copy, scale=gain_abs[:, t : t + 1])

        w2_bf = keep.tile([P, PACK, P, PACK], BF16, name="w2_bf", tag="x_plane", align_bytes=64)
        for t in (0, 1):
            nc.scalar.copy(
                w2_bf[:, t].rearrange("p (a c i) j -> p a c j i", c=2, i=4),
                w2_signed[:].rearrange("p j (a t c i) -> p t a c j i", t=PACK, c=2, i=4)[:, t],
            )
        for t in (2, 3):
            nc.gpsimd.tensor_scalar(
                w2_bf[:, t].rearrange("p (a c) j -> p a c j", c=8),
                w2_signed[:].rearrange("p j (a t c) -> p t a c j", t=PACK, c=8)[:, t],
                1.0,
                0.0,
                ALU.mult,
                ALU.add,
            )

        h_acc = [psum.tile([P, S], F32, name=f"h_acc{t}") for t in range(PACK)]
        h_win = [keep.tile([P, 2 * S], F32, name=f"h_win{t}", align_bytes=64) for t in range(PACK)]
        for t in range(PACK):
            nc.gpsimd.memset(h_win[t][:, S:], 0.0)
        z_plane = keep.tile([P, S], U8, name="z_plane", align_bytes=64)
        fetched = keep.tile([P, PACK, S], BF16, name="fetched", align_bytes=64)
        for t in range(PACK):
            for lo in (0, HALF):
                nc.vector.tensor_copy(fetched[:, t, lo : lo + HALF], y_win[t][:].indirect(entries(n1_t, lo, lo + HALF)))
        z_halves = [keep.tile([P, PACK, HALF], BF16, name=f"z_half{u}", align_bytes=64) for u in range(2)]
        for u in range(2):
            c = slice(u * HALF, (u + 1) * HALF)
            nc.vector.tensor_tensor(z_halves[u][:], fetched[:, :, c], y_bf[:, :, c], ALU.max)
        z_rows = [z_halves[0][:], z_halves[1][:, :, 0 : HALF // 2], z_halves[1][:, :, HALF // 2 :]]

        w2_codes = keep.tile([P, N], U32, name="w2_codes", tag=f"y_win{PACK - 1}", align_bytes=64)
        z_codes = keep.tile([P, S], U32, name="z_codes", align_bytes=64)
        z_bf = [keep.tile([P, (hi - lo) * PACK], BF16, name=f"z_bf{i}", align_bytes=64) for i, (lo, hi) in enumerate(Z_PIECES)]

        def weave(i):
            woven = z_bf[i][:].rearrange("p (c i t) -> p c t i", i=4, t=PACK)
            rows = z_rows[i].rearrange("p t (c i) -> p c t i", i=4)
            if i == len(Z_PIECES) - 1:
                nc.vector.tensor_copy(woven, rows)
            else:
                nc.scalar.copy(woven, rows)

        def quantise(i):
            lo, hi = Z_PIECES[i]
            nc.vector.quantize_mx(z_codes[:, lo:hi].bitcast(FP8X4), z_plane[:, lo:hi], z_bf[i][:])
            product(h_acc[0], w2_codes, w2_plane, 0, z_codes, z_plane, lo, hi)

        def h_half(t, lo):
            product(h_acc[t], w2_codes, w2_plane, t, z_codes, z_plane, lo, lo + HALF)
            nc.scalar.copy(h_win[t][:, lo : lo + HALF], h_acc[t][:, lo : lo + HALF])

        weave(0)
        weave(1)
        nc.vector.quantize_mx(w2_codes[:].bitcast(FP8X4), w2_plane[:], w2_bf[:].rearrange("p t m j -> p (t m j)"))
        quantise(0)
        weave(2)
        quantise(1)
        quantise(2)
        nc.scalar.copy(h_win[0][:, 0:S], h_acc[0][:])
        h_half(1, 0)
        h_half(1, HALF)

        def h_whole(t):
            product(h_acc[t], w2_codes, w2_plane, t, z_codes, z_plane, 0, S)
            nc.scalar.copy(h_win[t][:, 0:S], h_acc[t][:])

        h_whole(2)

        out_rows = out.rearrange("(a t c) n -> t a c n", t=PACK, c=8)
        halves = (slice(0, HALF), slice(HALF, S))
        other = [keep.tile([P, S], F32, name=f"other{t}", align_bytes=64) for t in range(PACK)]
        gate = [keep.tile([P, S], F32, name=f"gate{t}", align_bytes=64) for t in range(PACK)]
        res = [keep.tile([P, S], F32, name=f"res{t}", align_bytes=64) for t in range(PACK)]
        diff_first = keep.tile([P, S], F32, name="diff_first", align_bytes=64)
        diff = [diff_first[:]] + [h_win[t][:, S:] for t in range(PACK - 1)]
        for t in range(PACK - 1):
            nc.scalar.activation(gate[t][:], h_win[t][:].indirect(n3_t[:]), ACT.Sigmoid)
            if t == 0:
                h_whole(PACK - 1)
        for c in halves:
            nc.scalar.activation(gate[3][:, c], h_win[3][:].indirect(entries(n3_t, c.start, c.stop)), ACT.Sigmoid)
        for t in range(PACK):
            nc.vector.tensor_copy(other[t][:], h_win[t][:].indirect(n2_t[:]))
        nc.gpsimd.tensor_tensor(diff[0], h_win[0][:, 0:S], other[0][:], ALU.subtract)
        for t in (1, 2):
            nc.vector.tensor_tensor(diff[t], h_acc[t][:], other[t][:], ALU.subtract)
        for c in halves:
            nc.vector.tensor_tensor(diff[3][:, c], h_acc[3][:, c], other[3][:, c], ALU.subtract)
        for t in (0, 1):
            nc.gpsimd.tensor_tensor(res[t][:], diff[t], gate[t][:], ALU.mult)
            nc.sync.dma_start(out_rows[t], res[t][:])
        for t, c, engine in ((2, halves[0], nc.gpsimd), (2, halves[1], nc.vector), (3, halves[0], nc.vector), (3, halves[1], nc.vector)):
            engine.tensor_tensor(res[t][:, c], diff[t][:, c], gate[t][:, c], ALU.mult)
            nc.sync.dma_start(out_rows[t, :, :, c], res[t][:, c])
